import numpy as np
import ml_dtypes


def mxq(x, axis, fmt="e4m3"):
    dtype, down = {"e4m3": (ml_dtypes.float8_e4m3fn, 7), "e5m2": (ml_dtypes.float8_e5m2, 14)}[fmt]
    v = np.moveaxis(np.asarray(x, np.float32).astype(ml_dtypes.bfloat16).astype(np.float64), axis, -1)
    blocks = v.reshape(v.shape[:-1] + (-1, 32))
    amax = np.abs(blocks).max(-1, keepdims=True)
    byte = np.maximum(np.where(amax > 0, np.frexp(amax)[1] - 1 + 127, 0) - down, 1)
    scale = np.exp2(byte - 127.0)
    codes = (blocks / scale).astype(np.float32).astype(dtype).astype(np.float64)
    return np.moveaxis((codes * scale).reshape(v.shape), -1, axis)


WIDE = False


def mx_kscale(k):
    if not WIDE:
        return np.ones(k)
    levels = np.array([24, -24, 12, -12, 0])
    if k % 512:
        return np.exp2(np.random.permutation(np.resize(levels, k // 32))).repeat(32)
    a = np.empty((k // 512, 16))
    for p in range(k // 512):
        a[p, :8] = np.random.permutation(np.resize(levels, 8))
        for g in range(8):
            far = levels[np.abs(levels - a[p, g]) >= 10]
            a[p, g + 8] = far[np.random.randint(len(far))]
    return np.exp2(a.ravel()).repeat(32)


def f64(x):
    return np.asarray(x).astype(np.float64)


E2M1 = np.array([0.0, 0.5, 1.0, 1.5, 2.0, 3.0, 4.0, 6.0, -0.0, -0.5, -1.0, -1.5, -2.0, -3.0, -4.0, -6.0])


def pack_weight(w, fmt):
    k, n = w.shape
    w = f64(np.asarray(w, np.float32).astype(ml_dtypes.bfloat16)).reshape(k // 32, 32, n)
    amax = np.abs(w).max(1)
    if fmt == "e4m3":
        byte = np.frexp(amax)[1] - 1 + 127 - 7
    else:
        mant, ex = np.frexp(amax / 6.0)
        byte = np.where(mant > 0.5, ex, ex - 1) + 127
    byte = np.clip(np.where(amax > 0, byte, 1), 1, 254)
    scaled = (w * np.exp2(127.0 - byte)[:, None, :]).reshape(k, n).astype(np.float32)
    by_word = np.ascontiguousarray(scaled.reshape(k // 512, 128, 4, n).transpose(0, 1, 3, 2))
    if fmt == "e4m3":
        words = by_word.astype(ml_dtypes.float8_e4m3fn).view(np.uint8)
    else:
        c = by_word.astype(ml_dtypes.float4_e2m1fn).view(np.uint8) & 0xF
        words = (c[..., 0::2] | (c[..., 1::2] << 4)).reshape(k // 512, 128, 2 * n)
    return np.ascontiguousarray(words), np.ascontiguousarray(byte.astype(np.uint8).reshape(k // 512, 16, n))


def unpack_weight(words, scales, fmt):
    g, _, n = scales.shape
    words = np.ascontiguousarray(words).reshape(g, 128, n, -1)
    if fmt == "e4m3":
        vals = words.view(ml_dtypes.float8_e4m3fn).astype(np.float64)
    else:
        nib = np.empty((g, 128, n, 4), np.uint8)
        nib[..., 0::2] = words & 0xF
        nib[..., 1::2] = words >> 4
        vals = E2M1[nib]
    vals = vals * np.repeat(np.exp2(scales.astype(np.float64) - 127.0), 8, axis=1)[..., None]
    return vals.transpose(0, 1, 3, 2).reshape(g * 512, n)


K, F, T = 1024, 512, 1536


def setup_inputs():
    n = np.random.standard_normal
    s = mx_kscale(K)[:, None]
    v = n((K, F)) / np.sqrt(K)
    p_vs = pack_weight(v ** 2 / s ** 2, "e4m3")
    return {
        "x": (n((K, T)) * s).astype(np.float32),
        "v": (v / s).astype(np.float32),
        "vs_words": p_vs[0],
        "vs_scales": p_vs[1],
    }


def reference(x, v, vs_words, vs_scales):
    x_ = mxq(f64(x), 0, "e4m3")
    xs_ = mxq(f64(x) * f64(x), 0, "e4m3")
    v_ = mxq(f64(v), 0, "e4m3")
    vs_ = unpack_weight(vs_words, vs_scales, "e4m3")
    a = v_.T @ x_
    c = vs_.T @ xs_
    return 0.5 * (a * a - c)

@@ -1,0 +1,261 @@
+import math
+from contextlib import ExitStack
+
+import concourse.mybir as mybir
+
+K, F, T = 1024, 512, 1536
+FLOPS = 4 * K * F * T
+
+F32 = mybir.dt.float32
+BF16 = mybir.dt.bfloat16
+U32 = mybir.dt.uint32
+I32 = mybir.dt.int32
+U8 = mybir.dt.uint8
+FP8X4 = mybir.dt.float8_e4m3fn_x4
+ACT = mybir.ActivationFunctionType
+ALU = mybir.AluOpType
+
+P = 128
+PACK = 4
+K_PASS = P * PACK
+PASSES = K // K_PASS
+T_TILE = 512
+F_TILE = 128
+F_HALF = 256
+RUN = 4
+
+
+def tile_mix_fm_none_kernel(tc, x, v, vs_words, vs_scales, out):
+    nc = tc.nc
+    with ExitStack() as ctx:
+        keep = ctx.enter_context(tc.tile_pool(name="keep", bufs=1))
+        stage = ctx.enter_context(tc.tile_pool(name="stage", bufs=3))
+        psum = ctx.enter_context(tc.psum_pool(name="psum", bufs=4))
+        ctx.enter_context(tc.manual_schedule())
+
+        raw = {}
+        grouped = {}
+        codes = {}
+        scales = {}
+        squared = {}
+        banks = {}
+        vs_codes = {}
+
+        def load(key, src, g, c0, width):
+            raw[key] = keep.tile([P, PACK, width], F32, name="raw_%s" % key)
+            rows = src[g * K_PASS : (g + 1) * K_PASS, c0 : c0 + width]
+            nc.sync.dma_start(out=raw[key][:], in_=rows.rearrange("(p j) w -> p j w", j=PACK))
+
+        def views(key, kind):
+            width = raw[key].shape[2]
+            tile = stage.tile([P, width, PACK], BF16, name="grouped_%s" % kind, tag="grouped_%s" % kind, align_bytes=64)
+            grouped[(key, kind)] = tile
+            dst = tile[:].rearrange("p (c i) j -> p c j i", i=RUN)
+            src = raw[key][:].rearrange("p j (c i) -> p c j i", i=RUN)
+            return dst, src
+
+        def cast_vector(key):
+            dst, src = views(key, "plain")
+            nc.vector.tensor_copy(out=dst, in_=src)
+
+        def cast_scalar(key):
+            dst, src = views(key, "act")
+            nc.scalar.activation(out=dst, in_=src, func=ACT.Copy)
+
+        def square(key):
+            dst, src = views(key, "square")
+            nc.scalar.activation(out=dst, in_=src, func=ACT.Square)
+
+        def operand(name, width):
+            codes[name] = keep.tile([P, width], U32, name="codes_%s" % name, align_bytes=64)
+            scales[name] = keep.tile([P, width], U8, name="scales_%s" % name, align_bytes=64)
+
+        def quantize(key, kind, name, c0=0):
+            tile = grouped[(key, kind)]
+            width = tile.shape[1]
+            nc.vector.quantize_mx(
+                out=codes[name][:, c0 : c0 + width].bitcast(FP8X4),
+                scales=scales[name][:, c0 : c0 + width],
+                in_=tile[:].rearrange("p w j -> p (w j)"),
+            )
+
+        def a_pass(t, f, g):
+            if g == 0:
+                banks[("a", t, f)] = psum.tile([P, T_TILE], F32, name="bank_a", tag="bank_a")
+            vn = "v%d%d" % (f // 2, g)
+            cols = slice((f % 2) * F_TILE, (f % 2 + 1) * F_TILE)
+            xn = "x%d%d" % (t, g)
+            nc.tensor.matmul_mx(
+                out=banks[("a", t, f)][:],
+                lhsT=codes[vn][:, cols].bitcast(FP8X4),
+                lhsT_scale=scales[vn][:, cols],
+                rhs=codes[xn][:].bitcast(FP8X4),
+                rhs_scale=scales[xn][:],
+                start=(g == 0),
+                stop=(g == PASSES - 1),
+            )
+
+        def c_pass(t, f, g):
+            if g == 0:
+                banks[("c", t, f)] = psum.tile([P, T_TILE], F32, name="bank_c", tag="bank_c")
+            cols = slice(f * F_TILE, (f + 1) * F_TILE)
+            xn = "s%d%d" % (t, g)
+            nc.tensor.matmul_mx(
+                out=banks[("c", t, f)][:],
+                lhsT=vs_codes[f // 2][:, g, (f % 2) * F_TILE : (f % 2 + 1) * F_TILE].bitcast(FP8X4),
+                lhsT_scale=vs_plane[:, g, cols],
+                rhs=codes[xn][:].bitcast(FP8X4),
+                rhs_scale=scales[xn][:],
+                start=(g == 0),
+                stop=(g == PASSES - 1),
+            )
+
+        def square_a(t, f):
+            tile = stage.tile([P, T_TILE], F32, name="a_squared", tag="a_squared", bufs=6)
+            squared[(t, f)] = tile
+            nc.scalar.activation(out=tile[:], in_=banks[("a", t, f)][:], func=ACT.Square, scale=math.sqrt(0.5))
+
+        def finish(t, f):
+            result = keep.tile([P, T_TILE], F32, name="result_%d%d" % (t, f))
+            nc.vector.scalar_tensor_tensor(
+                out=result[:], in0=banks[("c", t, f)][:], scalar=-0.5, in1=squared[(t, f)][:], op0=ALU.mult, op1=ALU.add
+            )
+            nc.sync.dma_start(out=out[f * F_TILE : (f + 1) * F_TILE, t * T_TILE : (t + 1) * T_TILE], in_=result[:])
+
+        def load_vs_scales():
+            for q in range(4):
+                nc.sync.dma_start(
+                    out=vs_plane[32 * q : 32 * q + 4].bitcast(I32),
+                    in_=vs_scales[:, 4 * q : 4 * q + 4, :].rearrange("a r f -> r a f").bitcast(I32),
+                )
+
+        def load_vs_words(h):
+            vs_codes[h] = keep.tile([P, PASSES, F_HALF], U32, name="vs_codes_%d" % h, align_bytes=64)
+            words = vs_words[:, :, h * F_HALF : (h + 1) * F_HALF, :].rearrange("a p f i -> p a (f i)")
+            nc.sync.dma_start(out=vs_codes[h][:].bitcast(I32), in_=words.bitcast(I32))
+
+        for t in range(3):
+            for g in range(PASSES):
+                operand("x%d%d" % (t, g), T_TILE)
+                operand("s%d%d" % (t, g), T_TILE)
+        for h in range(2):
+            for g in range(PASSES):
+                operand("v%d%d" % (h, g), F_HALF)
+        vs_plane = keep.tile([P, PASSES, F], U8, align_bytes=64)
+
+        nc.vector.memset(vs_plane[:].rearrange("p a f -> p (a f)").bitcast(I32), 0)
+        warm_in = keep.tile([P, 8], F32)
+        warm_out = keep.tile([P, 8], F32)
+        nc.vector.memset(warm_in[:], 0.0)
+        nc.scalar.activation(out=warm_out[:], in_=warm_in[:], func=ACT.Square)
+
+        def load_x(t, g):
+            for h in (0, 1):
+                load("x%d%d%s" % (t, g, "ab"[h]), x, g, t * T_TILE + 256 * h, 256)
+        def qx(key):
+            quantize("x" + key, "plain", "x" + key[0:2], 256 * "ab".index(key[2]))
+        def qs(key):
+            quantize("x" + key, "square", "s" + key[0:2], 256 * "ab".index(key[2]))
+        def passes(kind, t, fs, gs):
+            for f in fs:
+                for g in gs:
+                    kind(t, f, g)
+        load_x(0, 0)
+        load("v00", v, 0, 0, F_HALF)
+        load_x(0, 1)
+        load("v01", v, 1, 0, F_HALF)
+        load_vs_scales()
+        load_vs_words(0)
+        load_x(1, 0)
+        load("v10", v, 0, F_HALF, F_HALF)
+        load_x(1, 1)
+        load("v11", v, 1, F_HALF, F_HALF)
+        load_vs_words(1)
+        load_x(2, 0)
+        load_x(2, 1)
+        def round_x(key):
+            square("x" + key)
+            cast_vector("x" + key)
+        round_x("00a")
+        round_x("00b")
+        qx("00a")
+        qs("00a")
+        cast_scalar("v00")
+        qx("00b")
+        qs("00b")
+        round_x("01a")
+        quantize("v00", "act", "v00")
+        passes(a_pass, 0, (0, 1), (0,))
+        qx("01a")
+        round_x("01b")
+        qs("01a")
+        qx("01b")
+        cast_scalar("v01")
+        qs("01b")
+        passes(c_pass, 0, (0, 1), (0, 1))
+        quantize("v01", "act", "v01")
+        passes(a_pass, 0, (0, 1), (1,))
+        round_x("10a")
+        square_a(0, 0)
+        round_x("10b")
+        qx("10a")
+        qs("10a")
+        qx("10b")
+        finish(0, 0)
+        square_a(0, 1)
+        cast_vector("v10")
+        qs("10b")
+        quantize("v10", "plain", "v10")
+        passes(a_pass, 1, (0, 1), (0,))
+        passes(c_pass, 1, (0, 1), (0,))
+        passes(a_pass, 0, (2, 3), (0,))
+        round_x("11a")
+        finish(0, 1)
+        qx("11a")
+        round_x("11b")
+        qs("11a")
+        qx("11b")
+        passes(a_pass, 1, (0, 1), (1,))
+        cast_scalar("v11")
+        qs("11b")
+        passes(c_pass, 1, (0, 1), (1,))
+        passes(c_pass, 0, (2, 3), (0, 1))
+        square_a(1, 0)
+        round_x("20a")
+        quantize("v11", "act", "v11")
+        passes(a_pass, 0, (2, 3), (1,))
+        finish(1, 0)
+        qx("20a")
+        square_a(1, 1)
+        square_a(0, 2)
+        passes(a_pass, 1, (2, 3), (0, 1))
+        round_x("20b")
+        qs("20a")
+        finish(1, 1)
+        qx("20b")
+        passes(c_pass, 1, (2, 3), (0, 1))
+        square_a(0, 3)
+        round_x("21a")
+        finish(0, 2)
+        qs("20b")
+        qx("21a")
+        passes(a_pass, 2, (0, 1), (0,))
+        passes(c_pass, 2, (0,), (0,))
+        square_a(1, 2)
+        round_x("21b")
+        finish(0, 3)
+        qx("21b")
+        qs("21a")
+        passes(a_pass, 2, (2,), (0,))
+        passes(c_pass, 2, (1,), (0,))
+        passes(a_pass, 2, (0, 1, 2), (1,))
+        square_a(1, 3)
+        finish(1, 2)
+        qs("21b")
+        finish(1, 3)
+        passes(c_pass, 2, (0, 1), (1,))
+        passes(a_pass, 2, (3,), (0, 1))
+        passes(c_pass, 2, (2, 3), (0, 1))
+        for f in range(4):
+            square_a(2, f)
+            finish(2, f)

@@ -22,7 +22,7 @@ PASSES = K // K_PASS
 T_TILE = 512
 F_TILE = 128
 F_HALF = 256
-RUN = 4
+RUN = 2
 
 
 def tile_mix_fm_none_kernel(tc, x, v, vs_words, vs_scales, out):
@@ -82,8 +82,8 @@ def tile_mix_fm_none_kernel(tc, x, v, vs_words, vs_scales, out):
         def a_pass(t, f, g):
             if g == 0:
                 banks[("a", t, f)] = psum.tile([P, T_TILE], F32, name="bank_a", tag="bank_a")
-            vn = "v%d%d" % (f // 2, g)
-            cols = slice((f % 2) * F_TILE, (f % 2 + 1) * F_TILE)
+            vn = "v%d" % g
+            cols = slice(f * F_TILE, (f + 1) * F_TILE)
             xn = "x%d%d" % (t, g)
             nc.tensor.matmul_mx(
                 out=banks[("a", t, f)][:],
@@ -124,7 +124,7 @@ def tile_mix_fm_none_kernel(tc, x, v, vs_words, vs_scales, out):
 
         def load_vs_scales():
             for q in range(4):
-                nc.sync.dma_start(
+                nc.scalar.dma_start(
                     out=vs_plane[32 * q : 32 * q + 4].bitcast(I32),
                     in_=vs_scales[:, 4 * q : 4 * q + 4, :].rearrange("a r f -> r a f").bitcast(I32),
                 )
@@ -138,124 +138,110 @@ def tile_mix_fm_none_kernel(tc, x, v, vs_words, vs_scales, out):
             for g in range(PASSES):
                 operand("x%d%d" % (t, g), T_TILE)
                 operand("s%d%d" % (t, g), T_TILE)
-        for h in range(2):
-            for g in range(PASSES):
-                operand("v%d%d" % (h, g), F_HALF)
+        for g in range(PASSES):
+            operand("v%d" % g, F)
         vs_plane = keep.tile([P, PASSES, F], U8, align_bytes=64)
 
         nc.vector.memset(vs_plane[:].rearrange("p a f -> p (a f)").bitcast(I32), 0)
+        load_vs_scales()
         warm_in = keep.tile([P, 8], F32)
         warm_out = keep.tile([P, 8], F32)
         nc.vector.memset(warm_in[:], 0.0)
         nc.scalar.activation(out=warm_out[:], in_=warm_in[:], func=ACT.Square)
 
         def load_x(t, g):
-            for h in (0, 1):
-                load("x%d%d%s" % (t, g, "ab"[h]), x, g, t * T_TILE + 256 * h, 256)
-        def qx(key):
-            quantize("x" + key, "plain", "x" + key[0:2], 256 * "ab".index(key[2]))
-        def qs(key):
-            quantize("x" + key, "square", "s" + key[0:2], 256 * "ab".index(key[2]))
+            load("x%d%d" % (t, g), x, g, t * T_TILE, T_TILE)
+        def load_v(h, g):
+            load("v%d%d" % (h, g), v, g, h * F_HALF, F_HALF)
+        def round_x(key):
+            square(key)
+            cast_vector(key)
+        def qx(t, g):
+            quantize("x%d%d" % (t, g), "plain", "x%d%d" % (t, g))
+        def qs(t, g):
+            quantize("x%d%d" % (t, g), "square", "s%d%d" % (t, g))
+        def qv(h, g, kind):
+            quantize("v%d%d" % (h, g), kind, "v%d" % g, h * F_HALF)
         def passes(kind, t, fs, gs):
             for f in fs:
                 for g in gs:
                     kind(t, f, g)
-        load_x(0, 0)
-        load("v00", v, 0, 0, F_HALF)
+        load("x00a", x, 0, 0, 256)
+        load("x00b", x, 0, 256, 256)
         load_x(0, 1)
-        load("v01", v, 1, 0, F_HALF)
-        load_vs_scales()
-        load_vs_words(0)
         load_x(1, 0)
-        load("v10", v, 0, F_HALF, F_HALF)
+        load_vs_words(0)
+        load_v(0, 0)
         load_x(1, 1)
-        load("v11", v, 1, F_HALF, F_HALF)
-        load_vs_words(1)
+        load_v(0, 1)
+        load_v(1, 0)
+        load_v(1, 1)
         load_x(2, 0)
+        load_vs_words(1)
         load_x(2, 1)
-        def round_x(key):
-            square("x" + key)
-            cast_vector("x" + key)
-        round_x("00a")
-        round_x("00b")
-        qx("00a")
-        qs("00a")
-        cast_scalar("v00")
-        qx("00b")
-        qs("00b")
-        round_x("01a")
-        quantize("v00", "act", "v00")
-        passes(a_pass, 0, (0, 1), (0,))
-        qx("01a")
-        round_x("01b")
-        qs("01a")
-        qx("01b")
-        cast_scalar("v01")
-        qs("01b")
+        round_x("x00a")
+        round_x("x00b")
+        quantize("x00a", "plain", "x00", 0)
+        quantize("x00a", "square", "s00", 0)
+        quantize("x00b", "plain", "x00", 256)
+        quantize("x00b", "square", "s00", 256)
+        round_x("x01")
+        qx(0, 1)
+        round_x("x10")
+        qs(0, 1)
+        qx(1, 0)
         passes(c_pass, 0, (0, 1), (0, 1))
-        quantize("v01", "act", "v01")
-        passes(a_pass, 0, (0, 1), (1,))
-        round_x("10a")
-        square_a(0, 0)
-        round_x("10b")
-        qx("10a")
-        qs("10a")
-        qx("10b")
-        finish(0, 0)
-        square_a(0, 1)
-        cast_vector("v10")
-        qs("10b")
-        quantize("v10", "plain", "v10")
-        passes(a_pass, 1, (0, 1), (0,))
+        cast_vector("v00")
+        qs(1, 0)
+        qv(0, 0, "plain")
         passes(c_pass, 1, (0, 1), (0,))
-        passes(a_pass, 0, (2, 3), (0,))
-        round_x("11a")
-        finish(0, 1)
-        qx("11a")
-        round_x("11b")
-        qs("11a")
-        qx("11b")
+        passes(a_pass, 0, (0, 1), (0,))
+        passes(a_pass, 1, (0, 1), (0,))
+        round_x("x11")
+        cast_vector("v01")
+        qx(1, 1)
+        qv(0, 1, "plain")
+        passes(a_pass, 0, (0, 1), (1,))
         passes(a_pass, 1, (0, 1), (1,))
-        cast_scalar("v11")
-        qs("11b")
+        cast_scalar("v10")
+        qs(1, 1)
         passes(c_pass, 1, (0, 1), (1,))
-        passes(c_pass, 0, (2, 3), (0, 1))
-        square_a(1, 0)
-        round_x("20a")
-        quantize("v11", "act", "v11")
-        passes(a_pass, 0, (2, 3), (1,))
-        finish(1, 0)
-        qx("20a")
-        square_a(1, 1)
-        square_a(0, 2)
+        cast_vector("v11")
+        qv(1, 0, "act")
+        qv(1, 1, "plain")
+        for t in (0, 1):
+            for f in (0, 1):
+                square_a(t, f)
+        passes(a_pass, 0, (2, 3), (0, 1))
         passes(a_pass, 1, (2, 3), (0, 1))
-        round_x("20b")
-        qs("20a")
+        finish(0, 0)
+        finish(0, 1)
+        passes(c_pass, 0, (2, 3), (0, 1))
+        round_x("x20")
+        finish(1, 0)
+        qx(2, 0)
         finish(1, 1)
-        qx("20b")
         passes(c_pass, 1, (2, 3), (0, 1))
+        square_a(0, 2)
         square_a(0, 3)
-        round_x("21a")
-        finish(0, 2)
-        qs("20b")
-        qx("21a")
         passes(a_pass, 2, (0, 1), (0,))
-        passes(c_pass, 2, (0,), (0,))
-        square_a(1, 2)
-        round_x("21b")
+        round_x("x21")
+        qs(2, 0)
+        qx(2, 1)
+        passes(a_pass, 2, (0, 1), (1,))
+        finish(0, 2)
         finish(0, 3)
-        qx("21b")
-        qs("21a")
-        passes(a_pass, 2, (2,), (0,))
-        passes(c_pass, 2, (1,), (0,))
-        passes(a_pass, 2, (0, 1, 2), (1,))
-        square_a(1, 3)
-        finish(1, 2)
-        qs("21b")
-        finish(1, 3)
+        passes(c_pass, 2, (0, 1), (0,))
+        square_a(1, 2)
+        passes(a_pass, 2, (2,), (0, 1))
+        qs(2, 1)
         passes(c_pass, 2, (0, 1), (1,))
+        square_a(1, 3)
         passes(a_pass, 2, (3,), (0, 1))
-        passes(c_pass, 2, (2, 3), (0, 1))
+        finish(1, 2)
+        passes(c_pass, 2, (2,), (0, 1))
+        finish(1, 3)
+        passes(c_pass, 2, (3,), (0, 1))
         for f in range(4):
             square_a(2, f)
             finish(2, f)

@@ -4,7 +4,7 @@ from contextlib import ExitStack
 import concourse.mybir as mybir
 
 K, F, T = 1024, 512, 1536
-FLOPS = 4 * K * F * T
+FLOPS = 2 * (2 * K * F * T)
 
 F32 = mybir.dt.float32
 BF16 = mybir.dt.bfloat16
@@ -19,112 +19,48 @@ P = 128
 PACK = 4
 K_PASS = P * PACK
 PASSES = K // K_PASS
+BOTH = range(PASSES)
 T_TILE = 512
 F_TILE = 128
-F_HALF = 256
+F_HALF = F // 2
+LOW, HIGH = (0, 1), (2, 3)
+QUADRANTS = 4
 RUN = 2
+ROUND_BUFS = 3
+SQUARE_BUFS = 6
+BANKS = 4
 
 
 def tile_mix_fm_none_kernel(tc, x, v, vs_words, vs_scales, out):
     nc = tc.nc
     with ExitStack() as ctx:
         keep = ctx.enter_context(tc.tile_pool(name="keep", bufs=1))
-        stage = ctx.enter_context(tc.tile_pool(name="stage", bufs=3))
-        psum = ctx.enter_context(tc.psum_pool(name="psum", bufs=4))
+        stage = ctx.enter_context(tc.tile_pool(name="stage", bufs=ROUND_BUFS))
+        psum = ctx.enter_context(tc.psum_pool(name="psum", bufs=BANKS))
         ctx.enter_context(tc.manual_schedule())
 
         raw = {}
-        grouped = {}
+        rounded = {}
         codes = {}
         scales = {}
-        squared = {}
-        banks = {}
         vs_codes = {}
+        banks = {}
+        half_a_squared = {}
 
-        def load(key, src, g, c0, width):
-            raw[key] = keep.tile([P, PACK, width], F32, name="raw_%s" % key)
+        def load(name, src, g, c0, width):
+            raw[name] = keep.tile([P, PACK, width], F32, name="raw_%s" % name)
             rows = src[g * K_PASS : (g + 1) * K_PASS, c0 : c0 + width]
-            nc.sync.dma_start(out=raw[key][:], in_=rows.rearrange("(p j) w -> p j w", j=PACK))
+            nc.sync.dma_start(out=raw[name][:], in_=rows.rearrange("(p j) w -> p j w", j=PACK))
 
-        def views(key, kind):
-            width = raw[key].shape[2]
-            tile = stage.tile([P, width, PACK], BF16, name="grouped_%s" % kind, tag="grouped_%s" % kind, align_bytes=64)
-            grouped[(key, kind)] = tile
-            dst = tile[:].rearrange("p (c i) j -> p c j i", i=RUN)
-            src = raw[key][:].rearrange("p j (c i) -> p c j i", i=RUN)
-            return dst, src
+        def load_x(t, g):
+            load("x%d%d" % (t, g), x, g, t * T_TILE, T_TILE)
 
-        def cast_vector(key):
-            dst, src = views(key, "plain")
-            nc.vector.tensor_copy(out=dst, in_=src)
-
-        def cast_scalar(key):
-            dst, src = views(key, "act")
-            nc.scalar.activation(out=dst, in_=src, func=ACT.Copy)
-
-        def square(key):
-            dst, src = views(key, "square")
-            nc.scalar.activation(out=dst, in_=src, func=ACT.Square)
-
-        def operand(name, width):
-            codes[name] = keep.tile([P, width], U32, name="codes_%s" % name, align_bytes=64)
-            scales[name] = keep.tile([P, width], U8, name="scales_%s" % name, align_bytes=64)
-
-        def quantize(key, kind, name, c0=0):
-            tile = grouped[(key, kind)]
-            width = tile.shape[1]
-            nc.vector.quantize_mx(
-                out=codes[name][:, c0 : c0 + width].bitcast(FP8X4),
-                scales=scales[name][:, c0 : c0 + width],
-                in_=tile[:].rearrange("p w j -> p (w j)"),
-            )
-
-        def a_pass(t, f, g):
-            if g == 0:
-                banks[("a", t, f)] = psum.tile([P, T_TILE], F32, name="bank_a", tag="bank_a")
-            vn = "v%d" % g
-            cols = slice(f * F_TILE, (f + 1) * F_TILE)
-            xn = "x%d%d" % (t, g)
-            nc.tensor.matmul_mx(
-                out=banks[("a", t, f)][:],
-                lhsT=codes[vn][:, cols].bitcast(FP8X4),
-                lhsT_scale=scales[vn][:, cols],
-                rhs=codes[xn][:].bitcast(FP8X4),
-                rhs_scale=scales[xn][:],
-                start=(g == 0),
-                stop=(g == PASSES - 1),
-            )
-
-        def c_pass(t, f, g):
-            if g == 0:
-                banks[("c", t, f)] = psum.tile([P, T_TILE], F32, name="bank_c", tag="bank_c")
-            cols = slice(f * F_TILE, (f + 1) * F_TILE)
-            xn = "s%d%d" % (t, g)
-            nc.tensor.matmul_mx(
-                out=banks[("c", t, f)][:],
-                lhsT=vs_codes[f // 2][:, g, (f % 2) * F_TILE : (f % 2 + 1) * F_TILE].bitcast(FP8X4),
-                lhsT_scale=vs_plane[:, g, cols],
-                rhs=codes[xn][:].bitcast(FP8X4),
-                rhs_scale=scales[xn][:],
-                start=(g == 0),
-                stop=(g == PASSES - 1),
-            )
-
-        def square_a(t, f):
-            tile = stage.tile([P, T_TILE], F32, name="a_squared", tag="a_squared", bufs=6)
-            squared[(t, f)] = tile
-            nc.scalar.activation(out=tile[:], in_=banks[("a", t, f)][:], func=ACT.Square, scale=math.sqrt(0.5))
-
-        def finish(t, f):
-            result = keep.tile([P, T_TILE], F32, name="result_%d%d" % (t, f))
-            nc.vector.scalar_tensor_tensor(
-                out=result[:], in0=banks[("c", t, f)][:], scalar=-0.5, in1=squared[(t, f)][:], op0=ALU.mult, op1=ALU.add
-            )
-            nc.sync.dma_start(out=out[f * F_TILE : (f + 1) * F_TILE, t * T_TILE : (t + 1) * T_TILE], in_=result[:])
+        def load_v(h, g):
+            load("v%d%d" % (h, g), v, g, h * F_HALF, F_HALF)
 
         def load_vs_scales():
-            for q in range(4):
-                nc.scalar.dma_start(
+            for q in range(QUADRANTS):
+                nc.sync.dma_start(
                     out=vs_plane[32 * q : 32 * q + 4].bitcast(I32),
                     in_=vs_scales[:, 4 * q : 4 * q + 4, :].rearrange("a r f -> r a f").bitcast(I32),
                 )
@@ -134,114 +70,179 @@ def tile_mix_fm_none_kernel(tc, x, v, vs_words, vs_scales, out):
             words = vs_words[:, :, h * F_HALF : (h + 1) * F_HALF, :].rearrange("a p f i -> p a (f i)")
             nc.sync.dma_start(out=vs_codes[h][:].bitcast(I32), in_=words.bitcast(I32))
 
-        for t in range(3):
-            for g in range(PASSES):
-                operand("x%d%d" % (t, g), T_TILE)
-                operand("s%d%d" % (t, g), T_TILE)
-        for g in range(PASSES):
-            operand("v%d" % g, F)
-        vs_plane = keep.tile([P, PASSES, F], U8, align_bytes=64)
+        def interleave_views(name, kind):
+            width = raw[name].shape[2]
+            tile = stage.tile([P, width, PACK], BF16, name="rounded_%s" % kind, tag="rounded_%s" % kind, align_bytes=64)
+            rounded[(name, kind)] = tile
+            dst = tile[:].rearrange("p (c i) j -> p c j i", i=RUN)
+            src = raw[name][:].rearrange("p j (c i) -> p c j i", i=RUN)
+            return dst, src
 
-        nc.vector.memset(vs_plane[:].rearrange("p a f -> p (a f)").bitcast(I32), 0)
-        load_vs_scales()
-        warm_in = keep.tile([P, 8], F32)
-        warm_out = keep.tile([P, 8], F32)
-        nc.vector.memset(warm_in[:], 0.0)
-        nc.scalar.activation(out=warm_out[:], in_=warm_in[:], func=ACT.Square)
+        def round_on_vector(name):
+            dst, src = interleave_views(name, "vector")
+            nc.vector.tensor_copy(out=dst, in_=src)
 
-        def load_x(t, g):
-            load("x%d%d" % (t, g), x, g, t * T_TILE, T_TILE)
-        def load_v(h, g):
-            load("v%d%d" % (h, g), v, g, h * F_HALF, F_HALF)
-        def round_x(key):
-            square(key)
-            cast_vector(key)
-        def qx(t, g):
-            quantize("x%d%d" % (t, g), "plain", "x%d%d" % (t, g))
-        def qs(t, g):
-            quantize("x%d%d" % (t, g), "square", "s%d%d" % (t, g))
-        def qv(h, g, kind):
+        def round_on_scalar(name):
+            dst, src = interleave_views(name, "scalar")
+            nc.scalar.activation(out=dst, in_=src, func=ACT.Copy)
+
+        def round_x_and_xs(name):
+            dst, src = interleave_views(name, "square")
+            nc.scalar.activation(out=dst, in_=src, func=ACT.Square)
+            round_on_vector(name)
+
+        def quantize(name, kind, operand, c0):
+            tile = rounded[(name, kind)]
+            width = tile.shape[1]
+            nc.vector.quantize_mx(
+                out=codes[operand][:, c0 : c0 + width].bitcast(FP8X4),
+                scales=scales[operand][:, c0 : c0 + width],
+                in_=tile[:].rearrange("p w j -> p (w j)"),
+            )
+
+        def quantize_x(t, g):
+            quantize("x%d%d" % (t, g), "vector", "x%d%d" % (t, g), 0)
+
+        def quantize_xs(t, g):
+            quantize("x%d%d" % (t, g), "square", "xs%d%d" % (t, g), 0)
+
+        def quantize_v(h, g, kind):
             quantize("v%d%d" % (h, g), kind, "v%d" % g, h * F_HALF)
-        def passes(kind, t, fs, gs):
-            for f in fs:
-                for g in gs:
-                    kind(t, f, g)
-        load("x00a", x, 0, 0, 256)
-        load("x00b", x, 0, 256, 256)
+
+        def mx_pass(product, t, f, g, weight_codes, weight_scales, moving):
+            if g == 0:
+                banks[(product, t, f)] = psum.tile([P, T_TILE], F32, name="bank_" + product, tag="bank_" + product)
+            nc.tensor.matmul_mx(
+                out=banks[(product, t, f)][:],
+                lhsT=weight_codes.bitcast(FP8X4),
+                lhsT_scale=weight_scales,
+                rhs=codes[moving][:].bitcast(FP8X4),
+                rhs_scale=scales[moving][:],
+                start=(g == 0),
+                stop=(g == PASSES - 1),
+            )
+
+        def a_passes(t, f_tiles, pass_list):
+            for f in f_tiles:
+                cols = slice(f * F_TILE, (f + 1) * F_TILE)
+                for g in pass_list:
+                    mx_pass("a", t, f, g, codes["v%d" % g][:, cols], scales["v%d" % g][:, cols], "x%d%d" % (t, g))
+
+        def c_passes(t, f_tiles, pass_list):
+            for f in f_tiles:
+                cols = slice(f * F_TILE, (f + 1) * F_TILE)
+                half, within = divmod(f * F_TILE, F_HALF)
+                for g in pass_list:
+                    words = vs_codes[half][:, g, within : within + F_TILE]
+                    mx_pass("c", t, f, g, words, vs_plane[:, g, cols], "xs%d%d" % (t, g))
+
+        def square_a(t, f):
+            tile = stage.tile([P, T_TILE], F32, name="half_a_squared", tag="half_a_squared", bufs=SQUARE_BUFS)
+            half_a_squared[(t, f)] = tile
+            nc.scalar.activation(out=tile[:], in_=banks[("a", t, f)][:], func=ACT.Square, scale=math.sqrt(0.5))
+
+        def finish(t, f):
+            result = keep.tile([P, T_TILE], F32, name="result_%d%d" % (t, f))
+            nc.vector.scalar_tensor_tensor(
+                out=result[:],
+                in0=banks[("c", t, f)][:],
+                scalar=-0.5,
+                in1=half_a_squared[(t, f)][:],
+                op0=ALU.mult,
+                op1=ALU.add,
+            )
+            nc.sync.dma_start(out=out[f * F_TILE : (f + 1) * F_TILE, t * T_TILE : (t + 1) * T_TILE], in_=result[:])
+
+        for t in range(T // T_TILE):
+            for g in BOTH:
+                for operand in ("x%d%d" % (t, g), "xs%d%d" % (t, g)):
+                    codes[operand] = keep.tile([P, T_TILE], U32, name="codes_" + operand, align_bytes=64)
+                    scales[operand] = keep.tile([P, T_TILE], U8, name="scales_" + operand, align_bytes=64)
+        for g in BOTH:
+            codes["v%d" % g] = keep.tile([P, F], U32, name="codes_v%d" % g, align_bytes=64)
+            scales["v%d" % g] = keep.tile([P, F], U8, name="scales_v%d" % g, align_bytes=64)
+        vs_plane = keep.tile([P, PASSES, F], U8, align_bytes=64)
+        nc.vector.memset(vs_plane[:].rearrange("p a f -> p (a f)").bitcast(I32), 0)
+
+        first_halves = (("x00_left", 0), ("x00_right", T_TILE // 2))
+        for name, c0 in first_halves:
+            load(name, x, 0, c0, T_TILE // 2)
+        load_vs_scales()
         load_x(0, 1)
         load_x(1, 0)
-        load_vs_words(0)
         load_v(0, 0)
         load_x(1, 1)
+        load_vs_words(0)
         load_v(0, 1)
         load_v(1, 0)
         load_v(1, 1)
         load_x(2, 0)
         load_vs_words(1)
         load_x(2, 1)
-        round_x("x00a")
-        round_x("x00b")
-        quantize("x00a", "plain", "x00", 0)
-        quantize("x00a", "square", "s00", 0)
-        quantize("x00b", "plain", "x00", 256)
-        quantize("x00b", "square", "s00", 256)
-        round_x("x01")
-        qx(0, 1)
-        round_x("x10")
-        qs(0, 1)
-        qx(1, 0)
-        passes(c_pass, 0, (0, 1), (0, 1))
-        cast_vector("v00")
-        qs(1, 0)
-        qv(0, 0, "plain")
-        passes(c_pass, 1, (0, 1), (0,))
-        passes(a_pass, 0, (0, 1), (0,))
-        passes(a_pass, 1, (0, 1), (0,))
-        round_x("x11")
-        cast_vector("v01")
-        qx(1, 1)
-        qv(0, 1, "plain")
-        passes(a_pass, 0, (0, 1), (1,))
-        passes(a_pass, 1, (0, 1), (1,))
-        cast_scalar("v10")
-        qs(1, 1)
-        passes(c_pass, 1, (0, 1), (1,))
-        cast_vector("v11")
-        qv(1, 0, "act")
-        qv(1, 1, "plain")
+
+        for name, c0 in first_halves:
+            round_x_and_xs(name)
+        for name, c0 in first_halves:
+            quantize(name, "vector", "x00", c0)
+            quantize(name, "square", "xs00", c0)
+        round_x_and_xs("x01")
+        quantize_x(0, 1)
+        round_x_and_xs("x10")
+        quantize_xs(0, 1)
+        quantize_x(1, 0)
+
+        round_on_scalar("v00")
+        quantize_xs(1, 0)
+        c_passes(0, LOW, BOTH)
+        round_x_and_xs("x11")
+        quantize_v(0, 0, "scalar")
         for t in (0, 1):
-            for f in (0, 1):
+            a_passes(t, LOW, (0,))
+        round_on_vector("v01")
+        quantize_x(1, 1)
+        quantize_v(0, 1, "vector")
+        for t in (0, 1):
+            a_passes(t, LOW, (1,))
+        round_on_scalar("v10")
+        quantize_xs(1, 1)
+        c_passes(1, LOW, BOTH)
+        round_on_vector("v11")
+        quantize_v(1, 0, "scalar")
+        quantize_v(1, 1, "vector")
+
+        for t in (0, 1):
+            for f in LOW:
                 square_a(t, f)
-        passes(a_pass, 0, (2, 3), (0, 1))
-        passes(a_pass, 1, (2, 3), (0, 1))
-        finish(0, 0)
-        finish(0, 1)
-        passes(c_pass, 0, (2, 3), (0, 1))
-        round_x("x20")
-        finish(1, 0)
-        qx(2, 0)
-        finish(1, 1)
-        passes(c_pass, 1, (2, 3), (0, 1))
-        square_a(0, 2)
-        square_a(0, 3)
-        passes(a_pass, 2, (0, 1), (0,))
-        round_x("x21")
-        qs(2, 0)
-        qx(2, 1)
-        passes(a_pass, 2, (0, 1), (1,))
-        finish(0, 2)
-        finish(0, 3)
-        passes(c_pass, 2, (0, 1), (0,))
-        square_a(1, 2)
-        passes(a_pass, 2, (2,), (0, 1))
-        qs(2, 1)
-        passes(c_pass, 2, (0, 1), (1,))
-        square_a(1, 3)
-        passes(a_pass, 2, (3,), (0, 1))
-        finish(1, 2)
-        passes(c_pass, 2, (2,), (0, 1))
-        finish(1, 3)
-        passes(c_pass, 2, (3,), (0, 1))
-        for f in range(4):
+        for t in (0, 1):
+            a_passes(t, HIGH, BOTH)
+        for f in LOW:
+            finish(0, f)
+        c_passes(0, HIGH, BOTH)
+        round_x_and_xs("x20")
+        finish(1, LOW[0])
+        quantize_x(2, 0)
+        finish(1, LOW[1])
+        c_passes(1, HIGH, BOTH)
+
+        for f in HIGH:
+            square_a(0, f)
+        a_passes(2, LOW, (0,))
+        round_x_and_xs("x21")
+        quantize_xs(2, 0)
+        quantize_x(2, 1)
+        a_passes(2, LOW, (1,))
+        for f in HIGH:
+            finish(0, f)
+        c_passes(2, LOW, (0,))
+        square_a(1, HIGH[0])
+        a_passes(2, HIGH[:1], BOTH)
+        quantize_xs(2, 1)
+        c_passes(2, LOW, (1,))
+        square_a(1, HIGH[1])
+        a_passes(2, HIGH[1:], BOTH)
+        for f in HIGH:
+            finish(1, f)
+            c_passes(2, (f,), BOTH)
+        for f in LOW + HIGH:
             square_a(2, f)
             finish(2, f)

@@ -25,7 +25,7 @@ F_TILE = 128
 F_HALF = F // 2
 LOW, HIGH = (0, 1), (2, 3)
 QUADRANTS = 4
-RUN = 2
+RUN = 4
 ROUND_BUFS = 3
 SQUARE_BUFS = 6
 BANKS = 4
@@ -164,9 +164,7 @@ def tile_mix_fm_none_kernel(tc, x, v, vs_words, vs_scales, out):
         vs_plane = keep.tile([P, PASSES, F], U8, align_bytes=64)
         nc.vector.memset(vs_plane[:].rearrange("p a f -> p (a f)").bitcast(I32), 0)
 
-        first_halves = (("x00_left", 0), ("x00_right", T_TILE // 2))
-        for name, c0 in first_halves:
-            load(name, x, 0, c0, T_TILE // 2)
+        load_x(0, 0)
         load_vs_scales()
         load_x(0, 1)
         load_x(1, 0)
@@ -180,12 +178,10 @@ def tile_mix_fm_none_kernel(tc, x, v, vs_words, vs_scales, out):
         load_vs_words(1)
         load_x(2, 1)
 
-        for name, c0 in first_halves:
-            round_x_and_xs(name)
-        for name, c0 in first_halves:
-            quantize(name, "vector", "x00", c0)
-            quantize(name, "square", "xs00", c0)
+        round_x_and_xs("x00")
+        quantize_x(0, 0)
         round_x_and_xs("x01")
+        quantize_xs(0, 0)
         quantize_x(0, 1)
         round_x_and_xs("x10")
         quantize_xs(0, 1)

import math
from contextlib import ExitStack

import concourse.mybir as mybir

K, F, T = 1024, 512, 1536
FLOPS = 2 * (2 * K * F * T)

F32 = mybir.dt.float32
BF16 = mybir.dt.bfloat16
U32 = mybir.dt.uint32
I32 = mybir.dt.int32
U8 = mybir.dt.uint8
FP8X4 = mybir.dt.float8_e4m3fn_x4
ACT = mybir.ActivationFunctionType
ALU = mybir.AluOpType

P = 128
PACK = 4
K_PASS = P * PACK
PASSES = K // K_PASS
BOTH = range(PASSES)
T_TILE = 512
F_TILE = 128
F_HALF = F // 2
LOW, HIGH = (0, 1), (2, 3)
QUADRANTS = 4
RUN = 4
ROUND_BUFS = 3
SQUARE_BUFS = 6
BANKS = 4


def tile_mix_fm_none_kernel(tc, x, v, vs_words, vs_scales, out):
    nc = tc.nc
    with ExitStack() as ctx:
        keep = ctx.enter_context(tc.tile_pool(name="keep", bufs=1))
        stage = ctx.enter_context(tc.tile_pool(name="stage", bufs=ROUND_BUFS))
        psum = ctx.enter_context(tc.psum_pool(name="psum", bufs=BANKS))
        ctx.enter_context(tc.manual_schedule())

        raw = {}
        rounded = {}
        codes = {}
        scales = {}
        vs_codes = {}
        banks = {}
        half_a_squared = {}

        def load(name, src, g, c0, width):
            raw[name] = keep.tile([P, PACK, width], F32, name="raw_%s" % name)
            rows = src[g * K_PASS : (g + 1) * K_PASS, c0 : c0 + width]
            nc.sync.dma_start(out=raw[name][:], in_=rows.rearrange("(p j) w -> p j w", j=PACK))

        def load_x(t, g):
            load("x%d%d" % (t, g), x, g, t * T_TILE, T_TILE)

        def load_v(h, g):
            load("v%d%d" % (h, g), v, g, h * F_HALF, F_HALF)

        def load_vs_scales():
            for q in range(QUADRANTS):
                nc.sync.dma_start(
                    out=vs_plane[32 * q : 32 * q + 4].bitcast(I32),
                    in_=vs_scales[:, 4 * q : 4 * q + 4, :].rearrange("a r f -> r a f").bitcast(I32),
                )

        def load_vs_words(h):
            vs_codes[h] = keep.tile([P, PASSES, F_HALF], U32, name="vs_codes_%d" % h, align_bytes=64)
            words = vs_words[:, :, h * F_HALF : (h + 1) * F_HALF, :].rearrange("a p f i -> p a (f i)")
            nc.sync.dma_start(out=vs_codes[h][:].bitcast(I32), in_=words.bitcast(I32))

        def interleave_views(name, kind):
            width = raw[name].shape[2]
            tile = stage.tile([P, width, PACK], BF16, name="rounded_%s" % kind, tag="rounded_%s" % kind, align_bytes=64)
            rounded[(name, kind)] = tile
            dst = tile[:].rearrange("p (c i) j -> p c j i", i=RUN)
            src = raw[name][:].rearrange("p j (c i) -> p c j i", i=RUN)
            return dst, src

        def round_on_vector(name):
            dst, src = interleave_views(name, "vector")
            nc.vector.tensor_copy(out=dst, in_=src)

        def round_on_scalar(name):
            dst, src = interleave_views(name, "scalar")
            nc.scalar.activation(out=dst, in_=src, func=ACT.Copy)

        def round_x_and_xs(name):
            dst, src = interleave_views(name, "square")
            nc.scalar.activation(out=dst, in_=src, func=ACT.Square)
            round_on_vector(name)

        def quantize(name, kind, operand, c0):
            tile = rounded[(name, kind)]
            width = tile.shape[1]
            nc.vector.quantize_mx(
                out=codes[operand][:, c0 : c0 + width].bitcast(FP8X4),
                scales=scales[operand][:, c0 : c0 + width],
                in_=tile[:].rearrange("p w j -> p (w j)"),
            )

        def quantize_x(t, g):
            quantize("x%d%d" % (t, g), "vector", "x%d%d" % (t, g), 0)

        def quantize_xs(t, g):
            quantize("x%d%d" % (t, g), "square", "xs%d%d" % (t, g), 0)

        def quantize_v(h, g, kind):
            quantize("v%d%d" % (h, g), kind, "v%d" % g, h * F_HALF)

        def mx_pass(product, t, f, g, weight_codes, weight_scales, moving):
            if g == 0:
                banks[(product, t, f)] = psum.tile([P, T_TILE], F32, name="bank_" + product, tag="bank_" + product)
            nc.tensor.matmul_mx(
                out=banks[(product, t, f)][:],
                lhsT=weight_codes.bitcast(FP8X4),
                lhsT_scale=weight_scales,
                rhs=codes[moving][:].bitcast(FP8X4),
                rhs_scale=scales[moving][:],
                start=(g == 0),
                stop=(g == PASSES - 1),
            )

        def a_passes(t, f_tiles, pass_list):
            for f in f_tiles:
                cols = slice(f * F_TILE, (f + 1) * F_TILE)
                for g in pass_list:
                    mx_pass("a", t, f, g, codes["v%d" % g][:, cols], scales["v%d" % g][:, cols], "x%d%d" % (t, g))

        def c_passes(t, f_tiles, pass_list):
            for f in f_tiles:
                cols = slice(f * F_TILE, (f + 1) * F_TILE)
                half, within = divmod(f * F_TILE, F_HALF)
                for g in pass_list:
                    words = vs_codes[half][:, g, within : within + F_TILE]
                    mx_pass("c", t, f, g, words, vs_plane[:, g, cols], "xs%d%d" % (t, g))

        def square_a(t, f):
            tile = stage.tile([P, T_TILE], F32, name="half_a_squared", tag="half_a_squared", bufs=SQUARE_BUFS)
            half_a_squared[(t, f)] = tile
            nc.scalar.activation(out=tile[:], in_=banks[("a", t, f)][:], func=ACT.Square, scale=math.sqrt(0.5))

        def finish(t, f):
            result = keep.tile([P, T_TILE], F32, name="result_%d%d" % (t, f))
            nc.vector.scalar_tensor_tensor(
                out=result[:],
                in0=banks[("c", t, f)][:],
                scalar=-0.5,
                in1=half_a_squared[(t, f)][:],
                op0=ALU.mult,
                op1=ALU.add,
            )
            nc.sync.dma_start(out=out[f * F_TILE : (f + 1) * F_TILE, t * T_TILE : (t + 1) * T_TILE], in_=result[:])

        for t in range(T // T_TILE):
            for g in BOTH:
                for operand in ("x%d%d" % (t, g), "xs%d%d" % (t, g)):
                    codes[operand] = keep.tile([P, T_TILE], U32, name="codes_" + operand, align_bytes=64)
                    scales[operand] = keep.tile([P, T_TILE], U8, name="scales_" + operand, align_bytes=64)
        for g in BOTH:
            codes["v%d" % g] = keep.tile([P, F], U32, name="codes_v%d" % g, align_bytes=64)
            scales["v%d" % g] = keep.tile([P, F], U8, name="scales_v%d" % g, align_bytes=64)
        vs_plane = keep.tile([P, PASSES, F], U8, align_bytes=64)
        nc.vector.memset(vs_plane[:].rearrange("p a f -> p (a f)").bitcast(I32), 0)

        load_x(0, 0)
        load_vs_scales()
        load_x(0, 1)
        load_x(1, 0)
        load_v(0, 0)
        load_x(1, 1)
        load_vs_words(0)
        load_v(0, 1)
        load_v(1, 0)
        load_v(1, 1)
        load_x(2, 0)
        load_vs_words(1)
        load_x(2, 1)

        round_x_and_xs("x00")
        quantize_x(0, 0)
        round_x_and_xs("x01")
        quantize_xs(0, 0)
        quantize_x(0, 1)
        round_x_and_xs("x10")
        quantize_xs(0, 1)
        quantize_x(1, 0)

        round_on_scalar("v00")
        quantize_xs(1, 0)
        c_passes(0, LOW, BOTH)
        round_x_and_xs("x11")
        quantize_v(0, 0, "scalar")
        for t in (0, 1):
            a_passes(t, LOW, (0,))
        round_on_vector("v01")
        quantize_x(1, 1)
        quantize_v(0, 1, "vector")
        for t in (0, 1):
            a_passes(t, LOW, (1,))
        round_on_scalar("v10")
        quantize_xs(1, 1)
        c_passes(1, LOW, BOTH)
        round_on_vector("v11")
        quantize_v(1, 0, "scalar")
        quantize_v(1, 1, "vector")

        for t in (0, 1):
            for f in LOW:
                square_a(t, f)
        for t in (0, 1):
            a_passes(t, HIGH, BOTH)
        for f in LOW:
            finish(0, f)
        c_passes(0, HIGH, BOTH)
        round_x_and_xs("x20")
        finish(1, LOW[0])
        quantize_x(2, 0)
        finish(1, LOW[1])
        c_passes(1, HIGH, BOTH)

        for f in HIGH:
            square_a(0, f)
        a_passes(2, LOW, (0,))
        round_x_and_xs("x21")
        quantize_xs(2, 0)
        quantize_x(2, 1)
        a_passes(2, LOW, (1,))
        for f in HIGH:
            finish(0, f)
        c_passes(2, LOW, (0,))
        square_a(1, HIGH[0])
        a_passes(2, HIGH[:1], BOTH)
        quantize_xs(2, 1)
        c_passes(2, LOW, (1,))
        square_a(1, HIGH[1])
        a_passes(2, HIGH[1:], BOTH)
        for f in HIGH:
            finish(1, f)
            c_passes(2, (f,), BOTH)
        for f in LOW + HIGH:
            square_a(2, f)
            finish(2, f)
